import numpy as np, ml_dtypes
CORES = [52,68,84,180,196,212,308,324,340]
N = 9
import mx_ref
NC, KB = 128, 1
BF = ml_dtypes.bfloat16
def cut(t, i, w=512):
    return t[:, w * i:w * i + w]
def term(a, B):
    return np.stack([mx_ref.matmul(mx_ref.quantize(cut(a, i)), B) for i in range(4)], axis=2).reshape(128, -1)
def setup_inputs(rng):
    def f(*shape):
        return mx_ref.flush((rng.standard_normal(shape, dtype=np.float32) * np.exp2(rng.integers(-2, 3, shape[:-1] + (1,)))).astype(BF))
    return {"a": f(N, 128, 4 * 512), "b": f(N, 128, KB * 4 * NC)}
def setup_inputs_blocks(rng):
    d = setup_inputs(rng)
    for k in ("a", "b"): d[k] = mx_ref.spread(d[k], rng, 2)
    return d
def setup_inputs_wide(rng):
    d = setup_inputs(rng)
    for k in ("a", "b"): d[k] = mx_ref.flush((d[k].astype(np.float32) * np.exp2(rng.integers(-4, 5, (N, 1, 1))).astype(np.float32)).astype(BF))
    return d
def setup_inputs_lossless(rng):
    a = np.zeros((N, 128, 4 * 128, 4), np.float32)
    for r in range(N):
        k = rng.integers(0, 512, size=4 * 128)
        a[r, k // 4, np.arange(4 * 128), k % 4] = 1.0
    size = np.repeat(2.0 ** rng.integers(-4, 5, size=(1, 1, (KB * 4 * NC) // 4)), 4, axis=2)
    b = rng.integers(-1, 2, size=(N, 128, KB * 4 * NC)) * size
    return {"a": a.reshape(N, 128, 4 * 512).astype(BF), "b": b.astype(np.float32).astype(BF)}
def reference(a, b):
    y = np.zeros((N, 128, KB * 4 * NC), np.float32)
    for k in range(KB):
        y[:, :, 4 * NC * k:4 * NC * k + 4 * NC] = mx_ref.total([term(a[r], mx_ref.quantize(cut(b[r], k, 4 * NC))) for r in range(N)])
    return {"y": y}

@@ -1,0 +1,208 @@
+from concourse.bass import DstId, RemoteDMATransfer
+from concourse.mybir import dt, AluOpType, ActivationFunctionType
+
+NC = 128
+NP = 4
+TW = NP * NC
+BANK = 512
+RELAY = True
+
+_Q, _U = "float8_e4m3fn_x4", "uint8"
+SCRATCH = {
+    "at": ("sbuf", [128, NP * TW], "bfloat16"), "bt": ("sbuf", [128, TW], "bfloat16"),
+    "aq": ("sbuf", [128, NP * NC], _Q), "asc": ("sbuf", [128, NP * NC], _U),
+    "bq": ("sbuf", [128, NC], _Q), "bs": ("sbuf", [128, NC], _U),
+    "zt": ("sbuf", [128, TW], "bfloat16"),
+    "ones": ("sbuf", [128, TW + NP], "bfloat16"), "dg": ("sbuf", [128, TW + NP], "bfloat16"),
+    "eq": ("sbuf", [128, NP * NC], _Q), "es": ("sbuf", [128, NP * NC], _U),
+    "h": ("sbuf", [128, TW], "bfloat16"),
+    "q1": ("sbuf", [128, NC], _Q), "s1": ("sbuf", [128, NC], _U),
+    "q2": ("sbuf", [128, NC], _Q), "s2": ("sbuf", [128, NC], _U),
+    "l0q": ("sbuf", [128, NC], _Q), "l0s": ("sbuf", [128, NC], _U),
+    "l1q": ("sbuf", [128, NC], _Q), "l1s": ("sbuf", [128, NC], _U),
+    "l2q": ("sbuf", [128, NC], _Q), "l2s": ("sbuf", [128, NC], _U),
+    "l3q": ("sbuf", [128, NC], _Q), "l3s": ("sbuf", [128, NC], _U),
+    "fq": ("sbuf", [128, NC], _Q), "fs": ("sbuf", [128, NC], _U),
+    "ysb": ("sbuf", [128, TW], "float32"),
+    "ps": ("psum", [128, 2 * NP * BANK], "float32"),
+}
+SEMAPHORES = (["z", "pre", "one", "sel", "ldb", "qb", "cp", "q1", "qe", "cp2", "q2", "rdy", "sent", "fa", "fb", "out", "st"]
+              + ["%s%d" % (n, i) for n in ("lda", "qa", "mm", "arr", "dec", "fin") for i in range(NP)])
+
+
+def _deal(topo, src, dsts):
+    common = topo.mask(src, dsts[0])
+    for d in dsts:
+        common &= topo.mask(src, d)
+    engs = [e for e in range(common.bit_length()) if (common >> e) & 1]
+    per = 1
+    while 2 * per * len(dsts) <= len(engs):
+        per *= 2
+    return per, [sum(1 << e for e in engs[j * per:(j + 1) * per]) for j in range(len(dsts))]
+
+
+def rank_program(g, core, T, topo):
+    if T.rank_of(core) is None:
+        return
+    S = T.sem
+    v, t, sc, sy = g.vector, g.tensor, g.scalar, g.sync
+    hosts = sorted(set(topo.host(c) for c in T.cores))
+    mem = {h: sorted((c for c in T.cores if topo.host(c) == h), key=topo.chip) for h in hosts}
+    mid = [h for h in hosts if all(topo.may_write(x, y) and topo.may_write(y, x)
+                                   for x in mem[h] for y in T.cores if x != y)][0]
+    outer = [h for h in hosts if h != mid]
+    my = topo.host(core)
+    is_mid = my == mid
+    k = mem[my].index(core)
+    P = len(mem[my])
+
+    def others(c):
+        return [x for x in mem[topo.host(c)] if x != c]
+
+    peers = others(core)
+    bnd = [NC * j // P for j in range(P + 1)]
+    W = max(bnd[j + 1] - bnd[j] for j in range(P))
+    lo, hi = bnd[k], bnd[k + 1]
+
+    def ready_list(c):
+        return others(c) + ([mem[h][mem[mid].index(c)] for h in outer] if topo.host(c) == mid else [])
+
+    land = [(T["l%dq" % n], T["l%ds" % n]) for n in range(4)]
+    sent = [0]
+
+    def send(items):
+        per, masks = _deal(topo, core, [it[0] for it in items])
+        trs = []
+        for it, m in zip(items, masks):
+            rid, pid = topo.addr(it[0], core)
+            if it[2] is None:
+                trs.append(RemoteDMATransfer(dst_ids=[DstId(rid=rid, pnc=pid)], dma_engine_mask=m, remote_sem=it[1]))
+            else:
+                trs.append(RemoteDMATransfer(dst_ids=[DstId(rid=rid, pnc=pid)], dma_engine_mask=m, remote_sem=it[1],
+                                             src=it[2], dst=it[3]))
+        g.remote_dma_fused(trs, local_sem=S.sent)
+        sent[0] += per * len(items)
+
+    def ship(items):
+        send([(d, m, src[0][:, a:b].bitcast(dt.uint8), dst[0][:, a:b].bitcast(dt.uint8)) for d, m, src, dst, a, b in items])
+        send([(d, m, src[1][:, a:b], dst[1][:, a:b]) for d, m, src, dst, a, b in items])
+
+    def bank(n, a=0, b=NC):
+        return T.ps[:, BANK * n + a:BANK * n + b]
+
+    def cols(i):
+        return slice(NC * i, NC * i + NC)
+
+    sy.dma_start(T.bt[:], T.b[:]).then_inc(S.ldb, 16)
+    for i in range(NP):
+        (sc if i % 2 == 0 else sy).dma_start(T.at[:, TW * i:TW * i + TW], T.a[:, TW * i:TW * i + TW]).then_inc(S["lda%d" % i], 16)
+
+    filled = land[:2] + ((land[2:] + [(T.fq, T.fs)]) if is_mid else [])
+    v.memset(T.zt[:], 0.0).then_inc(S.z, 1)
+    v.wait_ge(S.z, 1)
+    for q, s in filled:
+        v.quantize_mx(q[:], s[:], T.zt[:]).then_inc(S.pre, 1)
+    v.memset(T.ones[:], 1.0).then_inc(S.one, 1)
+    v.wait_ge(S.ldb, 16)
+    v.quantize_mx(T.bq[:], T.bs[:], T.bt[:]).then_inc(S.qb, 1)
+    for i in range(NP):
+        v.wait_ge(S["lda%d" % i], 16)
+        v.quantize_mx(T.aq[:, cols(i)], T.asc[:, cols(i)], T.at[:, TW * i:TW * i + TW]).then_inc(S["qa%d" % i], 1)
+
+    t.wait_ge(S.qb, 1)
+    for i in range(NP):
+        t.wait_ge(S["qa%d" % i], 1)
+        t.matmul_mx(bank(i), T.aq[:, cols(i)], T.asc[:, cols(i)], T.bq[:], T.bs[:], True, True).then_inc(S["mm%d" % i], 1)
+    for i in range(NP):
+        t.matmul_mx(bank(NP + i), T.aq[:, cols(i)], T.asc[:, cols(i)], T.bq[:], T.bs[:], True, False)
+
+    for i in range(NP):
+        sc.wait_ge(S["mm%d" % i], 1)
+        sc.activation(T.h[:, i:TW:NP], bank(i), ActivationFunctionType.Copy).then_inc(S.cp, 1)
+    v.wait_ge(S.cp, NP)
+    v.quantize_mx(T.q1[:], T.s1[:], T.h[:]).then_inc(S.q1, 1)
+
+    g.wait_ge(S.pre, len(filled))
+    send([(d, S.rdy, None, None) for d in ready_list(core)])
+    g.wait_ge(S.one, 1)
+    g.affine_select(T.dg[:], T.ones[:], [[1, TW + NP]], AluOpType.is_equal, 0.0, -(NP - 1), -NP).then_inc(S.sel, 1)
+    g.wait_ge(S.rdy, sum(_deal(topo, x, ready_list(x))[0] for x in T.cores if x != core and core in ready_list(x)))
+    g.wait_ge(S.q1, 1)
+    hop1 = []
+    for p in peers:
+        a = min(bnd[mem[my].index(p)], NC - W)
+        n = others(p).index(core)
+        hop1.append((p, S["arr%d" % n], (T.q1, T.s1), land[n], a, a + W))
+    ship(hop1)
+
+    v.wait_ge(S.sel, 1)
+    for i in range(NP):
+        v.quantize_mx(T.eq[:, cols(i)], T.es[:, cols(i)], T.dg[:, NP - 1 - i:NP - 1 - i + TW]).then_inc(S.qe, 1)
+
+    froms = [(p, others(p)) for p in peers] + ([(mem[h][k], [core]) for h in outer] if is_mid else [])
+    t.wait_ge(S.qe, NP)
+    for n, (x, dsts) in enumerate(froms):
+        t.wait_ge(S["arr%d" % n], 2 * _deal(topo, x, dsts)[0])
+        for i in range(NP):
+            last = n == len(froms) - 1
+            ins = t.matmul_mx(bank(NP + i), T.eq[:, cols(i)], T.es[:, cols(i)], land[n][0][:], land[n][1][:], False, last)
+            if last:
+                ins.then_inc(S["dec%d" % i], 1)
+
+    n_out = 0
+    v.wait_ge(S.q1, 1)
+    sc.wait_ge(S.q1, 1)
+    for i in range(NP):
+        e = v if i % 2 == 0 else sc
+        e.wait_ge(S["dec%d" % i], 1)
+        if i % 2 == 0:
+            v.tensor_copy(T.h[:, NP * lo + i:NP * hi:NP], bank(NP + i, lo, hi)).then_inc(S.cp2, 1)
+        else:
+            sc.activation(T.h[:, NP * lo + i:NP * hi:NP], bank(NP + i, lo, hi), ActivationFunctionType.Copy).then_inc(S.cp2, 1)
+    v.wait_ge(S.cp2, NP)
+    v.quantize_mx(T.q2[:], T.s2[:], T.h[:]).then_inc(S.q2, 1)
+    if is_mid:
+        for i in range(NP):
+            if i % 2 == 0:
+                v.tensor_copy(T.ysb[:, NP * lo + i:NP * hi:NP], bank(NP + i, lo, hi)).then_inc(S.out, 1)
+            else:
+                sc.activation(T.ysb[:, NP * lo + i:NP * hi:NP], bank(NP + i, lo, hi), ActivationFunctionType.Copy).then_inc(S.out, 1)
+            n_out += 1
+
+    F = (T.fq, T.fs)
+    g.wait_ge(S.q2, 1)
+    if not is_mid:
+        ship([(mem[mid][k], S["arr%d" % (2 + outer.index(my))], (T.q2, T.s2), land[2 + outer.index(my)], lo, hi)])
+        if RELAY:
+            g.wait_ge(S.fa, 2 * _deal(topo, mem[mid][k], [mem[h][k] for h in outer])[0])
+            ship([(p, S.fb, F, F, lo, hi) for p in peers])
+    elif RELAY:
+        ship([(mem[h][k], S.fa, (T.q2, T.s2), F, lo, hi) for h in outer])
+        ship([(p, S.fb, (T.q2, T.s2), F, lo, hi) for p in peers])
+    else:
+        ship([(d, S.fb, (T.q2, T.s2), F, lo, hi) for d in T.cores if d != core])
+
+    if RELAY:
+        if not is_mid:
+            t.wait_ge(S.fa, 2 * _deal(topo, mem[mid][k], [mem[h][k] for h in outer])[0])
+        t.wait_ge(S.fb, sum(2 * _deal(topo, p, others(p))[0] for p in peers))
+    else:
+        t.wait_ge(S.fb, sum(2 * _deal(topo, x, [d for d in T.cores if d != x])[0] for x in mem[mid] if x != core))
+    t.wait_ge(S.cp, NP)
+    for i in range(NP):
+        t.matmul_mx(bank(i), T.eq[:, cols(i)], T.es[:, cols(i)], T.fq[:], T.fs[:], True, True).then_inc(S["fin%d" % i], 1)
+
+    spans = [(a, b) for a, b in ((0, lo), (hi, NC)) if b > a] if is_mid else [(0, NC)]
+    for i in range(NP):
+        e = v if i % 2 == 0 else sc
+        e.wait_ge(S["fin%d" % i], 1)
+        for a, b in spans:
+            if i % 2 == 0:
+                v.tensor_copy(T.ysb[:, NP * a + i:NP * b:NP], bank(i, a, b)).then_inc(S.out, 1)
+            else:
+                sc.activation(T.ysb[:, NP * a + i:NP * b:NP], bank(i, a, b), ActivationFunctionType.Copy).then_inc(S.out, 1)
+            n_out += 1
+    sy.wait_ge(S.out, n_out)
+    sy.dma_start(T.y[:], T.ysb[:]).then_inc(S.st, 16)
+    sy.wait_ge(S.st, 16)
+    g.wait_ge(S.sent, sent[0])

@@ -5,7 +5,6 @@ NC = 128
 NP = 4
 TW = NP * NC
 BANK = 512
-RELAY = True
 
 _Q, _U = "float8_e4m3fn_x4", "uint8"
 SCRATCH = {
@@ -22,12 +21,17 @@ SCRATCH = {
     "l1q": ("sbuf", [128, NC], _Q), "l1s": ("sbuf", [128, NC], _U),
     "l2q": ("sbuf", [128, NC], _Q), "l2s": ("sbuf", [128, NC], _U),
     "l3q": ("sbuf", [128, NC], _Q), "l3s": ("sbuf", [128, NC], _U),
-    "fq": ("sbuf", [128, NC], _Q), "fs": ("sbuf", [128, NC], _U),
+    "f0q": ("sbuf", [128, NC], _Q), "f0s": ("sbuf", [128, NC], _U),
+    "f1q": ("sbuf", [128, NC], _Q), "f1s": ("sbuf", [128, NC], _U),
+    "f2q": ("sbuf", [128, NC], _Q), "f2s": ("sbuf", [128, NC], _U),
+    "q3": ("sbuf", [128, NC], _Q), "s3": ("sbuf", [128, NC], _U),
+    "h2": ("sbuf", [128, TW], "bfloat16"),
     "ysb": ("sbuf", [128, TW], "float32"),
     "ps": ("psum", [128, 2 * NP * BANK], "float32"),
 }
-SEMAPHORES = (["z", "pre", "one", "sel", "ldb", "qb", "cp", "q1", "qe", "cp2", "q2", "rdy", "sent", "fa", "fb", "out", "st"]
-              + ["%s%d" % (n, i) for n in ("lda", "qa", "mm", "arr", "dec", "fin") for i in range(NP)])
+SEMAPHORES = (["z", "pre", "one", "sel", "ldb", "qb", "cp", "q1", "qe", "cp2", "q2", "cp3", "q3", "rdy", "sent",
+               "fa1", "fa2", "f0", "f1", "f2", "out", "st"]
+              + ["%s%d" % (n, i) for n in ("lda", "qa", "mm", "arr", "dec", "own", "fin") for i in range(NP)])
 
 
 def _deal(topo, src, dsts):
@@ -97,9 +101,12 @@ def rank_program(g, core, T, topo):
     for i in range(NP):
         (sc if i % 2 == 0 else sy).dma_start(T.at[:, TW * i:TW * i + TW], T.a[:, TW * i:TW * i + TW]).then_inc(S["lda%d" % i], 16)
 
-    filled = land[:2] + ((land[2:] + [(T.fq, T.fs)]) if is_mid else [])
+    F0, F1, F2 = (T.f0q, T.f0s), (T.f1q, T.f1s), (T.f2q, T.f2s)
+    Q2, Q3 = (T.q2, T.s2), (T.q3, T.s3)
+    filled = land[:2] + [F0] + (land[2:] if is_mid else [])
     v.memset(T.zt[:], 0.0).then_inc(S.z, 1)
-    v.wait_ge(S.z, 1)
+    v.memset(T.h2[:], 0.0).then_inc(S.z, 1)
+    v.wait_ge(S.z, 2)
     for q, s in filled:
         v.quantize_mx(q[:], s[:], T.zt[:]).then_inc(S.pre, 1)
     v.memset(T.ones[:], 1.0).then_inc(S.one, 1)
@@ -139,68 +146,102 @@ def rank_program(g, core, T, topo):
     for i in range(NP):
         v.quantize_mx(T.eq[:, cols(i)], T.es[:, cols(i)], T.dg[:, NP - 1 - i:NP - 1 - i + TW]).then_inc(S.qe, 1)
 
-    froms = [(p, others(p)) for p in peers] + ([(mem[h][k], [core]) for h in outer] if is_mid else [])
+    def dec(n, i, tile, start, stop):
+        return t.matmul_mx(bank(n), T.eq[:, cols(i)], T.es[:, cols(i)], tile[0][:], tile[1][:], start, stop)
+
+    def copy(i, out, in_, sem):
+        if i % 2 == 0:
+            v.tensor_copy(out, in_).then_inc(sem, 1)
+        else:
+            sc.activation(out, in_, ActivationFunctionType.Copy).then_inc(sem, 1)
+
+    def got(x, dsts):
+        return 2 * _deal(topo, x, dsts)[0]
+
     t.wait_ge(S.qe, NP)
-    for n, (x, dsts) in enumerate(froms):
-        t.wait_ge(S["arr%d" % n], 2 * _deal(topo, x, dsts)[0])
+    for n, p in enumerate(peers):
+        t.wait_ge(S["arr%d" % n], got(p, others(p)))
         for i in range(NP):
-            last = n == len(froms) - 1
-            ins = t.matmul_mx(bank(NP + i), T.eq[:, cols(i)], T.es[:, cols(i)], land[n][0][:], land[n][1][:], False, last)
+            last = n == len(peers) - 1
+            ins = dec(NP + i, i, land[n], False, last)
             if last:
                 ins.then_inc(S["dec%d" % i], 1)
 
     n_out = 0
-    v.wait_ge(S.q1, 1)
-    sc.wait_ge(S.q1, 1)
+    sc.wait_ge(S.z, 2)
     for i in range(NP):
-        e = v if i % 2 == 0 else sc
-        e.wait_ge(S["dec%d" % i], 1)
-        if i % 2 == 0:
-            v.tensor_copy(T.h[:, NP * lo + i:NP * hi:NP], bank(NP + i, lo, hi)).then_inc(S.cp2, 1)
-        else:
-            sc.activation(T.h[:, NP * lo + i:NP * hi:NP], bank(NP + i, lo, hi), ActivationFunctionType.Copy).then_inc(S.cp2, 1)
+        (v if i % 2 == 0 else sc).wait_ge(S["dec%d" % i], 1)
+        copy(i, T.h2[:, NP * lo + i:NP * hi:NP], bank(NP + i, lo, hi), S.cp2)
     v.wait_ge(S.cp2, NP)
-    v.quantize_mx(T.q2[:], T.s2[:], T.h[:]).then_inc(S.q2, 1)
-    if is_mid:
-        for i in range(NP):
-            if i % 2 == 0:
-                v.tensor_copy(T.ysb[:, NP * lo + i:NP * hi:NP], bank(NP + i, lo, hi)).then_inc(S.out, 1)
-            else:
-                sc.activation(T.ysb[:, NP * lo + i:NP * hi:NP], bank(NP + i, lo, hi), ActivationFunctionType.Copy).then_inc(S.out, 1)
-            n_out += 1
+    v.quantize_mx(T.q2[:], T.s2[:], T.h2[:]).then_inc(S.q2, 1)
 
-    F = (T.fq, T.fs)
+    mk = mem[mid][k]
+    same_k = [mem[h][k] for h in outer]
     g.wait_ge(S.q2, 1)
     if not is_mid:
-        ship([(mem[mid][k], S["arr%d" % (2 + outer.index(my))], (T.q2, T.s2), land[2 + outer.index(my)], lo, hi)])
-        if RELAY:
-            g.wait_ge(S.fa, 2 * _deal(topo, mem[mid][k], [mem[h][k] for h in outer])[0])
-            ship([(p, S.fb, F, F, lo, hi) for p in peers])
-    elif RELAY:
-        ship([(mem[h][k], S.fa, (T.q2, T.s2), F, lo, hi) for h in outer])
-        ship([(p, S.fb, (T.q2, T.s2), F, lo, hi) for p in peers])
+        o = outer.index(my)
+        ship([(mk, S["arr%d" % (2 + o)], Q2, land[2 + o], lo, hi)])
+        ship([(p, S.f0, Q2, F0, lo, hi) for p in peers])
+        g.wait_ge(S.fa1, got(mk, same_k))
+        ship([(p, S.f1, F1, F1, lo, hi) for p in peers])
+        g.wait_ge(S.fa2, got(mk, same_k))
+        ship([(p, S.f2, F2, F2, lo, hi) for p in peers])
     else:
-        ship([(d, S.fb, (T.q2, T.s2), F, lo, hi) for d in T.cores if d != core])
+        ship([(d, S.fa1, Q2, F1, lo, hi) for d in same_k])
+        for o, h in enumerate(outer):
+            g.wait_ge(S["arr%d" % (2 + o)], got(mem[h][k], [core]))
+        far = [land[2 + (len(outer) - 1 - o)] for o in range(len(outer))]
+        ship([(mem[h][k], S.fa2, far[o], F2, lo, hi) for o, h in enumerate(outer)])
+        g.wait_ge(S.q3, 1)
+        ship([(p, S.f0, Q3, F0, lo, hi) for p in peers])
 
-    if RELAY:
-        if not is_mid:
-            t.wait_ge(S.fa, 2 * _deal(topo, mem[mid][k], [mem[h][k] for h in outer])[0])
-        t.wait_ge(S.fb, sum(2 * _deal(topo, p, others(p))[0] for p in peers))
-    else:
-        t.wait_ge(S.fb, sum(2 * _deal(topo, x, [d for d in T.cores if d != x])[0] for x in mem[mid] if x != core))
+    n_f0 = sum(got(p, others(p)) for p in peers)
     t.wait_ge(S.cp, NP)
+    t.wait_ge(S.q2, 1)
     for i in range(NP):
-        t.matmul_mx(bank(i), T.eq[:, cols(i)], T.es[:, cols(i)], T.fq[:], T.fs[:], True, True).then_inc(S["fin%d" % i], 1)
+        dec(i, i, Q2, True, False)
+    if not is_mid:
+        t.wait_ge(S.f0, n_f0)
+        for i in range(NP):
+            dec(i, i, F0, False, False)
+        t.wait_ge(S.fa1, got(mk, same_k))
+        t.wait_ge(S.f1, n_f0)
+        for i in range(NP):
+            dec(i, i, F1, False, False)
+        t.wait_ge(S.fa2, got(mk, same_k))
+        t.wait_ge(S.f2, n_f0)
+        for i in range(NP):
+            dec(i, i, F2, False, True).then_inc(S["fin%d" % i], 1)
+        fb = 0
+    else:
+        for o, h in enumerate(outer):
+            t.wait_ge(S["arr%d" % (2 + o)], got(mem[h][k], [core]))
+            for i in range(NP):
+                last = o == len(outer) - 1
+                ins = dec(i, i, land[2 + o], False, last)
+                if last:
+                    ins.then_inc(S["own%d" % i], 1)
+        v.wait_ge(S.q2, 1)
+        sc.wait_ge(S.q2, 1)
+        for i in range(NP):
+            (v if i % 2 == 0 else sc).wait_ge(S["own%d" % i], 1)
+            copy(i, T.h2[:, NP * lo + i:NP * hi:NP], bank(i, lo, hi), S.cp3)
+        v.wait_ge(S.cp3, NP)
+        v.quantize_mx(T.q3[:], T.s3[:], T.h2[:]).then_inc(S.q3, 1)
+        for i in range(NP):
+            copy(i, T.ysb[:, NP * lo + i:NP * hi:NP], bank(i, lo, hi), S.out)
+            n_out += 1
+        t.wait_ge(S.cp2, NP)
+        t.wait_ge(S.f0, n_f0)
+        for i in range(NP):
+            dec(NP + i, i, F0, True, True).then_inc(S["fin%d" % i], 1)
+        fb = NP
 
     spans = [(a, b) for a, b in ((0, lo), (hi, NC)) if b > a] if is_mid else [(0, NC)]
     for i in range(NP):
-        e = v if i % 2 == 0 else sc
-        e.wait_ge(S["fin%d" % i], 1)
+        (v if i % 2 == 0 else sc).wait_ge(S["fin%d" % i], 1)
         for a, b in spans:
-            if i % 2 == 0:
-                v.tensor_copy(T.ysb[:, NP * a + i:NP * b:NP], bank(i, a, b)).then_inc(S.out, 1)
-            else:
-                sc.activation(T.ysb[:, NP * a + i:NP * b:NP], bank(i, a, b), ActivationFunctionType.Copy).then_inc(S.out, 1)
+            copy(i, T.ysb[:, NP * a + i:NP * b:NP], bank(fb + i, a, b), S.out)
             n_out += 1
     sy.wait_ge(S.out, n_out)
     sy.dma_start(T.y[:], T.ysb[:]).then_inc(S.st, 16)

@@ -30,7 +30,7 @@ SCRATCH = {
     "ps": ("psum", [128, 2 * NP * BANK], "float32"),
 }
 SEMAPHORES = (["z", "pre", "one", "sel", "ldb", "qb", "cp", "q1", "qe", "cp2", "q2", "cp3", "q3", "rdy", "sent",
-               "fa1", "fa2", "f0", "f1", "f2", "out", "st"]
+               "fa1c", "fa1p", "fa2c", "fa2p", "a2c", "a2p", "a3c", "a3p", "f0", "f1", "f2", "out", "st"]
               + ["%s%d" % (n, i) for n in ("lda", "qa", "mm", "arr", "dec", "own", "fin") for i in range(NP)])
 
 
@@ -87,9 +87,15 @@ def rank_program(g, core, T, topo):
         g.remote_dma_fused(trs, local_sem=S.sent)
         sent[0] += per * len(items)
 
-    def ship(items):
+    def codes(items):
         send([(d, m, src[0][:, a:b].bitcast(dt.uint8), dst[0][:, a:b].bitcast(dt.uint8)) for d, m, src, dst, a, b in items])
+
+    def planes(items):
         send([(d, m, src[1][:, a:b], dst[1][:, a:b]) for d, m, src, dst, a, b in items])
+
+    def ship(items):
+        codes(items)
+        planes(items)
 
     def bank(n, a=0, b=NC):
         return T.ps[:, BANK * n + a:BANK * n + b]
@@ -105,11 +111,11 @@ def rank_program(g, core, T, topo):
     Q2, Q3 = (T.q2, T.s2), (T.q3, T.s3)
     filled = land[:2] + [F0] + (land[2:] if is_mid else [])
     v.memset(T.zt[:], 0.0).then_inc(S.z, 1)
-    v.memset(T.h2[:], 0.0).then_inc(S.z, 1)
-    v.wait_ge(S.z, 2)
+    v.wait_ge(S.z, 1)
     for q, s in filled:
         v.quantize_mx(q[:], s[:], T.zt[:]).then_inc(S.pre, 1)
     v.memset(T.ones[:], 1.0).then_inc(S.one, 1)
+    v.memset(T.h2[:], 0.0).then_inc(S.z, 1)
     v.wait_ge(S.ldb, 16)
     v.quantize_mx(T.bq[:], T.bs[:], T.bt[:]).then_inc(S.qb, 1)
     for i in range(NP):
@@ -135,12 +141,11 @@ def rank_program(g, core, T, topo):
     g.affine_select(T.dg[:], T.ones[:], [[1, TW + NP]], AluOpType.is_equal, 0.0, -(NP - 1), -NP).then_inc(S.sel, 1)
     g.wait_ge(S.rdy, sum(_deal(topo, x, ready_list(x))[0] for x in T.cores if x != core and core in ready_list(x)))
     g.wait_ge(S.q1, 1)
-    hop1 = []
-    for p in peers:
+    for d in range(1, P):
+        p = mem[my][(k + d) % P]
         a = min(bnd[mem[my].index(p)], NC - W)
         n = others(p).index(core)
-        hop1.append((p, S["arr%d" % n], (T.q1, T.s1), land[n], a, a + W))
-    ship(hop1)
+        ship([(p, S["arr%d" % n], (T.q1, T.s1), land[n], a, a + W)])
 
     v.wait_ge(S.sel, 1)
     for i in range(NP):
@@ -155,20 +160,26 @@ def rank_program(g, core, T, topo):
         else:
             sc.activation(out, in_, ActivationFunctionType.Copy).then_inc(sem, 1)
 
+    def one(x, dsts):
+        return _deal(topo, x, dsts)[0]
+
     def got(x, dsts):
-        return 2 * _deal(topo, x, dsts)[0]
+        return 2 * one(x, dsts)
 
     t.wait_ge(S.qe, NP)
-    for n, p in enumerate(peers):
-        t.wait_ge(S["arr%d" % n], got(p, others(p)))
+    for d in range(1, P):
+        p = mem[my][(k - d) % P]
+        n = peers.index(p)
+        t.wait_ge(S["arr%d" % n], got(p, [core]))
         for i in range(NP):
-            last = n == len(peers) - 1
+            last = d == P - 1
             ins = dec(NP + i, i, land[n], False, last)
             if last:
                 ins.then_inc(S["dec%d" % i], 1)
 
     n_out = 0
     sc.wait_ge(S.z, 2)
+    v.wait_ge(S.z, 2)
     for i in range(NP):
         (v if i % 2 == 0 else sc).wait_ge(S["dec%d" % i], 1)
         copy(i, T.h2[:, NP * lo + i:NP * hi:NP], bank(NP + i, lo, hi), S.cp2)
@@ -177,21 +188,28 @@ def rank_program(g, core, T, topo):
 
     mk = mem[mid][k]
     same_k = [mem[h][k] for h in outer]
+    one_mk = one(mk, same_k)
     g.wait_ge(S.q2, 1)
     if not is_mid:
         o = outer.index(my)
-        ship([(mk, S["arr%d" % (2 + o)], Q2, land[2 + o], lo, hi)])
+        codes([(mk, S["a%dc" % (2 + o)], Q2, land[2 + o], lo, hi)])
+        planes([(mk, S["a%dp" % (2 + o)], Q2, land[2 + o], lo, hi)])
         ship([(p, S.f0, Q2, F0, lo, hi) for p in peers])
-        g.wait_ge(S.fa1, got(mk, same_k))
-        ship([(p, S.f1, F1, F1, lo, hi) for p in peers])
-        g.wait_ge(S.fa2, got(mk, same_k))
-        ship([(p, S.f2, F2, F2, lo, hi) for p in peers])
+        for tile, sem, n in ((F1, S.f1, 1), (F2, S.f2, 2)):
+            g.wait_ge(S["fa%dc" % n], one_mk)
+            codes([(p, sem, tile, tile, lo, hi) for p in peers])
+            g.wait_ge(S["fa%dp" % n], one_mk)
+            planes([(p, sem, tile, tile, lo, hi) for p in peers])
     else:
-        ship([(d, S.fa1, Q2, F1, lo, hi) for d in same_k])
-        for o, h in enumerate(outer):
-            g.wait_ge(S["arr%d" % (2 + o)], got(mem[h][k], [core]))
+        codes([(d, S.fa1c, Q2, F1, lo, hi) for d in same_k])
+        planes([(d, S.fa1p, Q2, F1, lo, hi) for d in same_k])
         far = [land[2 + (len(outer) - 1 - o)] for o in range(len(outer))]
-        ship([(mem[h][k], S.fa2, far[o], F2, lo, hi) for o, h in enumerate(outer)])
+        for o, h in enumerate(outer):
+            g.wait_ge(S["a%dc" % (2 + o)], one(mem[h][k], [core]))
+        codes([(mem[h][k], S.fa2c, far[o], F2, lo, hi) for o, h in enumerate(outer)])
+        for o, h in enumerate(outer):
+            g.wait_ge(S["a%dp" % (2 + o)], one(mem[h][k], [core]))
+        planes([(mem[h][k], S.fa2p, far[o], F2, lo, hi) for o, h in enumerate(outer)])
         g.wait_ge(S.q3, 1)
         ship([(p, S.f0, Q3, F0, lo, hi) for p in peers])
 
@@ -204,18 +222,21 @@ def rank_program(g, core, T, topo):
         t.wait_ge(S.f0, n_f0)
         for i in range(NP):
             dec(i, i, F0, False, False)
-        t.wait_ge(S.fa1, got(mk, same_k))
+        t.wait_ge(S.fa1c, one_mk)
+        t.wait_ge(S.fa1p, one_mk)
         t.wait_ge(S.f1, n_f0)
         for i in range(NP):
             dec(i, i, F1, False, False)
-        t.wait_ge(S.fa2, got(mk, same_k))
+        t.wait_ge(S.fa2c, one_mk)
+        t.wait_ge(S.fa2p, one_mk)
         t.wait_ge(S.f2, n_f0)
         for i in range(NP):
             dec(i, i, F2, False, True).then_inc(S["fin%d" % i], 1)
         fb = 0
     else:
         for o, h in enumerate(outer):
-            t.wait_ge(S["arr%d" % (2 + o)], got(mem[h][k], [core]))
+            t.wait_ge(S["a%dc" % (2 + o)], one(mem[h][k], [core]))
+            t.wait_ge(S["a%dp" % (2 + o)], one(mem[h][k], [core]))
             for i in range(NP):
                 last = o == len(outer) - 1
                 ins = dec(i, i, land[2 + o], False, last)

from concourse.bass import DstId, RemoteDMATransfer
from concourse.mybir import dt, AluOpType, ActivationFunctionType

NC = 128
NP = 4
TW = NP * NC
BANK = 512

_Q, _U = "float8_e4m3fn_x4", "uint8"
SCRATCH = {
    "at": ("sbuf", [128, NP * TW], "bfloat16"), "bt": ("sbuf", [128, TW], "bfloat16"),
    "aq": ("sbuf", [128, NP * NC], _Q), "asc": ("sbuf", [128, NP * NC], _U),
    "bq": ("sbuf", [128, NC], _Q), "bs": ("sbuf", [128, NC], _U),
    "zt": ("sbuf", [128, TW], "bfloat16"),
    "ones": ("sbuf", [128, TW + NP], "bfloat16"), "dg": ("sbuf", [128, TW + NP], "bfloat16"),
    "eq": ("sbuf", [128, NP * NC], _Q), "es": ("sbuf", [128, NP * NC], _U),
    "h": ("sbuf", [128, TW], "bfloat16"),
    "q1": ("sbuf", [128, NC], _Q), "s1": ("sbuf", [128, NC], _U),
    "q2": ("sbuf", [128, NC], _Q), "s2": ("sbuf", [128, NC], _U),
    "l0q": ("sbuf", [128, NC], _Q), "l0s": ("sbuf", [128, NC], _U),
    "l1q": ("sbuf", [128, NC], _Q), "l1s": ("sbuf", [128, NC], _U),
    "l2q": ("sbuf", [128, NC], _Q), "l2s": ("sbuf", [128, NC], _U),
    "l3q": ("sbuf", [128, NC], _Q), "l3s": ("sbuf", [128, NC], _U),
    "f0q": ("sbuf", [128, NC], _Q), "f0s": ("sbuf", [128, NC], _U),
    "f1q": ("sbuf", [128, NC], _Q), "f1s": ("sbuf", [128, NC], _U),
    "f2q": ("sbuf", [128, NC], _Q), "f2s": ("sbuf", [128, NC], _U),
    "q3": ("sbuf", [128, NC], _Q), "s3": ("sbuf", [128, NC], _U),
    "h2": ("sbuf", [128, TW], "bfloat16"),
    "ysb": ("sbuf", [128, TW], "float32"),
    "ps": ("psum", [128, 2 * NP * BANK], "float32"),
}
SEMAPHORES = (["z", "pre", "one", "sel", "ldb", "qb", "cp", "q1", "qe", "cp2", "q2", "cp3", "q3", "rdy", "sent",
               "fa1c", "fa1p", "fa2c", "fa2p", "a2c", "a2p", "a3c", "a3p", "f0", "f1", "f2", "out", "st"]
              + ["%s%d" % (n, i) for n in ("lda", "qa", "mm", "arr", "dec", "own", "fin") for i in range(NP)])


def _deal(topo, src, dsts):
    common = topo.mask(src, dsts[0])
    for d in dsts:
        common &= topo.mask(src, d)
    engs = [e for e in range(common.bit_length()) if (common >> e) & 1]
    per = 1
    while 2 * per * len(dsts) <= len(engs):
        per *= 2
    return per, [sum(1 << e for e in engs[j * per:(j + 1) * per]) for j in range(len(dsts))]


def rank_program(g, core, T, topo):
    if T.rank_of(core) is None:
        return
    S = T.sem
    v, t, sc, sy = g.vector, g.tensor, g.scalar, g.sync
    hosts = sorted(set(topo.host(c) for c in T.cores))
    mem = {h: sorted((c for c in T.cores if topo.host(c) == h), key=topo.chip) for h in hosts}
    mid = [h for h in hosts if all(topo.may_write(x, y) and topo.may_write(y, x)
                                   for x in mem[h] for y in T.cores if x != y)][0]
    outer = [h for h in hosts if h != mid]
    my = topo.host(core)
    is_mid = my == mid
    k = mem[my].index(core)
    P = len(mem[my])

    def others(c):
        return [x for x in mem[topo.host(c)] if x != c]

    peers = others(core)
    bnd = [NC * j // P for j in range(P + 1)]
    W = max(bnd[j + 1] - bnd[j] for j in range(P))
    lo, hi = bnd[k], bnd[k + 1]

    def ready_list(c):
        return others(c) + ([mem[h][mem[mid].index(c)] for h in outer] if topo.host(c) == mid else [])

    land = [(T["l%dq" % n], T["l%ds" % n]) for n in range(4)]
    sent = [0]

    def send(items):
        per, masks = _deal(topo, core, [it[0] for it in items])
        trs = []
        for it, m in zip(items, masks):
            rid, pid = topo.addr(it[0], core)
            if it[2] is None:
                trs.append(RemoteDMATransfer(dst_ids=[DstId(rid=rid, pnc=pid)], dma_engine_mask=m, remote_sem=it[1]))
            else:
                trs.append(RemoteDMATransfer(dst_ids=[DstId(rid=rid, pnc=pid)], dma_engine_mask=m, remote_sem=it[1],
                                             src=it[2], dst=it[3]))
        g.remote_dma_fused(trs, local_sem=S.sent)
        sent[0] += per * len(items)

    def codes(items):
        send([(d, m, src[0][:, a:b].bitcast(dt.uint8), dst[0][:, a:b].bitcast(dt.uint8)) for d, m, src, dst, a, b in items])

    def planes(items):
        send([(d, m, src[1][:, a:b], dst[1][:, a:b]) for d, m, src, dst, a, b in items])

    def ship(items):
        codes(items)
        planes(items)

    def bank(n, a=0, b=NC):
        return T.ps[:, BANK * n + a:BANK * n + b]

    def cols(i):
        return slice(NC * i, NC * i + NC)

    sy.dma_start(T.bt[:], T.b[:]).then_inc(S.ldb, 16)
    for i in range(NP):
        (sc if i % 2 == 0 else sy).dma_start(T.at[:, TW * i:TW * i + TW], T.a[:, TW * i:TW * i + TW]).then_inc(S["lda%d" % i], 16)

    F0, F1, F2 = (T.f0q, T.f0s), (T.f1q, T.f1s), (T.f2q, T.f2s)
    Q2, Q3 = (T.q2, T.s2), (T.q3, T.s3)
    filled = land[:2] + [F0] + (land[2:] if is_mid else [])
    v.memset(T.zt[:], 0.0).then_inc(S.z, 1)
    v.wait_ge(S.z, 1)
    for q, s in filled:
        v.quantize_mx(q[:], s[:], T.zt[:]).then_inc(S.pre, 1)
    v.memset(T.ones[:], 1.0).then_inc(S.one, 1)
    v.memset(T.h2[:], 0.0).then_inc(S.z, 1)
    v.wait_ge(S.ldb, 16)
    v.quantize_mx(T.bq[:], T.bs[:], T.bt[:]).then_inc(S.qb, 1)
    for i in range(NP):
        v.wait_ge(S["lda%d" % i], 16)
        v.quantize_mx(T.aq[:, cols(i)], T.asc[:, cols(i)], T.at[:, TW * i:TW * i + TW]).then_inc(S["qa%d" % i], 1)

    t.wait_ge(S.qb, 1)
    for i in range(NP):
        t.wait_ge(S["qa%d" % i], 1)
        t.matmul_mx(bank(i), T.aq[:, cols(i)], T.asc[:, cols(i)], T.bq[:], T.bs[:], True, True).then_inc(S["mm%d" % i], 1)
    for i in range(NP):
        t.matmul_mx(bank(NP + i), T.aq[:, cols(i)], T.asc[:, cols(i)], T.bq[:], T.bs[:], True, False)

    for i in range(NP):
        sc.wait_ge(S["mm%d" % i], 1)
        sc.activation(T.h[:, i:TW:NP], bank(i), ActivationFunctionType.Copy).then_inc(S.cp, 1)
    v.wait_ge(S.cp, NP)
    v.quantize_mx(T.q1[:], T.s1[:], T.h[:]).then_inc(S.q1, 1)

    g.wait_ge(S.pre, len(filled))
    send([(d, S.rdy, None, None) for d in ready_list(core)])
    g.wait_ge(S.one, 1)
    g.affine_select(T.dg[:], T.ones[:], [[1, TW + NP]], AluOpType.is_equal, 0.0, -(NP - 1), -NP).then_inc(S.sel, 1)
    g.wait_ge(S.rdy, sum(_deal(topo, x, ready_list(x))[0] for x in T.cores if x != core and core in ready_list(x)))
    g.wait_ge(S.q1, 1)
    for d in range(1, P):
        p = mem[my][(k + d) % P]
        a = min(bnd[mem[my].index(p)], NC - W)
        n = others(p).index(core)
        ship([(p, S["arr%d" % n], (T.q1, T.s1), land[n], a, a + W)])

    v.wait_ge(S.sel, 1)
    for i in range(NP):
        v.quantize_mx(T.eq[:, cols(i)], T.es[:, cols(i)], T.dg[:, NP - 1 - i:NP - 1 - i + TW]).then_inc(S.qe, 1)

    def dec(n, i, tile, start, stop):
        return t.matmul_mx(bank(n), T.eq[:, cols(i)], T.es[:, cols(i)], tile[0][:], tile[1][:], start, stop)

    def copy(i, out, in_, sem):
        if i % 2 == 0:
            v.tensor_copy(out, in_).then_inc(sem, 1)
        else:
            sc.activation(out, in_, ActivationFunctionType.Copy).then_inc(sem, 1)

    def one(x, dsts):
        return _deal(topo, x, dsts)[0]

    def got(x, dsts):
        return 2 * one(x, dsts)

    t.wait_ge(S.qe, NP)
    for d in range(1, P):
        p = mem[my][(k - d) % P]
        n = peers.index(p)
        t.wait_ge(S["arr%d" % n], got(p, [core]))
        for i in range(NP):
            last = d == P - 1
            ins = dec(NP + i, i, land[n], False, last)
            if last:
                ins.then_inc(S["dec%d" % i], 1)

    n_out = 0
    sc.wait_ge(S.z, 2)
    v.wait_ge(S.z, 2)
    for i in range(NP):
        (v if i % 2 == 0 else sc).wait_ge(S["dec%d" % i], 1)
        copy(i, T.h2[:, NP * lo + i:NP * hi:NP], bank(NP + i, lo, hi), S.cp2)
    v.wait_ge(S.cp2, NP)
    v.quantize_mx(T.q2[:], T.s2[:], T.h2[:]).then_inc(S.q2, 1)

    mk = mem[mid][k]
    same_k = [mem[h][k] for h in outer]
    one_mk = one(mk, same_k)
    g.wait_ge(S.q2, 1)
    if not is_mid:
        o = outer.index(my)
        codes([(mk, S["a%dc" % (2 + o)], Q2, land[2 + o], lo, hi)])
        planes([(mk, S["a%dp" % (2 + o)], Q2, land[2 + o], lo, hi)])
        ship([(p, S.f0, Q2, F0, lo, hi) for p in peers])
        for tile, sem, n in ((F1, S.f1, 1), (F2, S.f2, 2)):
            g.wait_ge(S["fa%dc" % n], one_mk)
            codes([(p, sem, tile, tile, lo, hi) for p in peers])
            g.wait_ge(S["fa%dp" % n], one_mk)
            planes([(p, sem, tile, tile, lo, hi) for p in peers])
    else:
        codes([(d, S.fa1c, Q2, F1, lo, hi) for d in same_k])
        planes([(d, S.fa1p, Q2, F1, lo, hi) for d in same_k])
        far = [land[2 + (len(outer) - 1 - o)] for o in range(len(outer))]
        for o, h in enumerate(outer):
            g.wait_ge(S["a%dc" % (2 + o)], one(mem[h][k], [core]))
        codes([(mem[h][k], S.fa2c, far[o], F2, lo, hi) for o, h in enumerate(outer)])
        for o, h in enumerate(outer):
            g.wait_ge(S["a%dp" % (2 + o)], one(mem[h][k], [core]))
        planes([(mem[h][k], S.fa2p, far[o], F2, lo, hi) for o, h in enumerate(outer)])
        g.wait_ge(S.q3, 1)
        ship([(p, S.f0, Q3, F0, lo, hi) for p in peers])

    n_f0 = sum(got(p, others(p)) for p in peers)
    t.wait_ge(S.cp, NP)
    t.wait_ge(S.q2, 1)
    for i in range(NP):
        dec(i, i, Q2, True, False)
    if not is_mid:
        t.wait_ge(S.f0, n_f0)
        for i in range(NP):
            dec(i, i, F0, False, False)
        t.wait_ge(S.fa1c, one_mk)
        t.wait_ge(S.fa1p, one_mk)
        t.wait_ge(S.f1, n_f0)
        for i in range(NP):
            dec(i, i, F1, False, False)
        t.wait_ge(S.fa2c, one_mk)
        t.wait_ge(S.fa2p, one_mk)
        t.wait_ge(S.f2, n_f0)
        for i in range(NP):
            dec(i, i, F2, False, True).then_inc(S["fin%d" % i], 1)
        fb = 0
    else:
        for o, h in enumerate(outer):
            t.wait_ge(S["a%dc" % (2 + o)], one(mem[h][k], [core]))
            t.wait_ge(S["a%dp" % (2 + o)], one(mem[h][k], [core]))
            for i in range(NP):
                last = o == len(outer) - 1
                ins = dec(i, i, land[2 + o], False, last)
                if last:
                    ins.then_inc(S["own%d" % i], 1)
        v.wait_ge(S.q2, 1)
        sc.wait_ge(S.q2, 1)
        for i in range(NP):
            (v if i % 2 == 0 else sc).wait_ge(S["own%d" % i], 1)
            copy(i, T.h2[:, NP * lo + i:NP * hi:NP], bank(i, lo, hi), S.cp3)
        v.wait_ge(S.cp3, NP)
        v.quantize_mx(T.q3[:], T.s3[:], T.h2[:]).then_inc(S.q3, 1)
        for i in range(NP):
            copy(i, T.ysb[:, NP * lo + i:NP * hi:NP], bank(i, lo, hi), S.out)
            n_out += 1
        t.wait_ge(S.cp2, NP)
        t.wait_ge(S.f0, n_f0)
        for i in range(NP):
            dec(NP + i, i, F0, True, True).then_inc(S["fin%d" % i], 1)
        fb = NP

    spans = [(a, b) for a, b in ((0, lo), (hi, NC)) if b > a] if is_mid else [(0, NC)]
    for i in range(NP):
        (v if i % 2 == 0 else sc).wait_ge(S["fin%d" % i], 1)
        for a, b in spans:
            copy(i, T.ysb[:, NP * a + i:NP * b:NP], bank(fb + i, a, b), S.out)
            n_out += 1
    sy.wait_ge(S.out, n_out)
    sy.dma_start(T.y[:], T.ysb[:]).then_inc(S.st, 16)
    sy.wait_ge(S.st, 16)
    g.wait_ge(S.sent, sent[0])
